import numpy as np
import ml_dtypes


def mxq(x, axis, fmt="e4m3"):
    dtype, down = {"e4m3": (ml_dtypes.float8_e4m3fn, 7), "e5m2": (ml_dtypes.float8_e5m2, 14)}[fmt]
    v = np.moveaxis(np.asarray(x, np.float32).astype(ml_dtypes.bfloat16).astype(np.float64), axis, -1)
    blocks = v.reshape(v.shape[:-1] + (-1, 32))
    amax = np.abs(blocks).max(-1, keepdims=True)
    byte = np.maximum(np.where(amax > 0, np.frexp(amax)[1] - 1 + 127, 0) - down, 1)
    scale = np.exp2(byte - 127.0)
    codes = (blocks / scale).astype(np.float32).astype(dtype).astype(np.float64)
    return np.moveaxis((codes * scale).reshape(v.shape), -1, axis)


WIDE = False


def mx_kscale(k):
    if not WIDE:
        return np.ones(k)
    levels = np.array([10, -10, 5, -5, 0])
    if k % 512:
        return np.exp2(np.random.permutation(np.resize(levels, k // 32))).repeat(32)
    a = np.empty((k // 512, 16))
    for p in range(k // 512):
        a[p, :8] = np.random.permutation(np.resize(levels, 8))
        for g in range(8):
            far = levels[np.abs(levels - a[p, g]) >= 10]
            a[p, g + 8] = far[np.random.randint(len(far))]
    return np.exp2(a.ravel()).repeat(32)


def f64(x):
    return np.asarray(x).astype(np.float64)


def striped(idx):
    return np.tile(np.asarray(idx).reshape(-1, 16).T, (8, 1)).astype(np.uint16)


def unstriped(offs):
    return offs[:16].T.reshape(-1).astype(np.int64)


E2M1 = np.array([0.0, 0.5, 1.0, 1.5, 2.0, 3.0, 4.0, 6.0, -0.0, -0.5, -1.0, -1.5, -2.0, -3.0, -4.0, -6.0])


def pack_weight(w, fmt):
    k, n = w.shape
    w = f64(np.asarray(w, np.float32).astype(ml_dtypes.bfloat16)).reshape(k // 32, 32, n)
    amax = np.abs(w).max(1)
    if fmt == "e4m3":
        byte = np.frexp(amax)[1] - 1 + 127 - 7
    else:
        mant, ex = np.frexp(amax / 6.0)
        byte = np.where(mant > 0.5, ex, ex - 1) + 127
    byte = np.clip(np.where(amax > 0, byte, 1), 1, 254)
    scaled = (w * np.exp2(127.0 - byte)[:, None, :]).reshape(k, n).astype(np.float32)
    by_word = np.ascontiguousarray(scaled.reshape(k // 512, 128, 4, n).transpose(0, 1, 3, 2))
    if fmt == "e4m3":
        words = by_word.astype(ml_dtypes.float8_e4m3fn).view(np.uint8)
    else:
        c = by_word.astype(ml_dtypes.float4_e2m1fn).view(np.uint8) & 0xF
        words = (c[..., 0::2] | (c[..., 1::2] << 4)).reshape(k // 512, 128, 2 * n)
    return np.ascontiguousarray(words), np.ascontiguousarray(byte.astype(np.uint8).reshape(k // 512, 16, n))


def unpack_weight(words, scales, fmt):
    g, _, n = scales.shape
    words = np.ascontiguousarray(words).reshape(g, 128, n, -1)
    if fmt == "e4m3":
        vals = words.view(ml_dtypes.float8_e4m3fn).astype(np.float64)
    else:
        nib = np.empty((g, 128, n, 4), np.uint8)
        nib[..., 0::2] = words & 0xF
        nib[..., 1::2] = words >> 4
        vals = E2M1[nib]
    vals = vals * np.repeat(np.exp2(scales.astype(np.float64) - 127.0), 8, axis=1)[..., None]
    return vals.transpose(0, 1, 3, 2).reshape(g * 512, n)


K, T, J, N = 1024, 2048, 512, 512


def setup_inputs():
    n = np.random.standard_normal
    idx = np.random.permutation(T)[:J]
    idx2 = np.random.permutation(T)[:J]
    fk = mx_kscale(K)
    xtp = pack_weight(n((K, T)) / fk[:, None], "e4m3")
    wbp = pack_weight(n((K, N)) * 1 / np.sqrt(K) * fk[:, None], "e2m1")
    return {
        "xt_words": xtp[0],
        "xt_scales": xtp[1],
        "wa": (n((K, N)) * 1 / np.sqrt(K) * fk[:, None]).astype(np.float32),
        "wb_words": wbp[0],
        "wb_scales": wbp[1],
        "offs": striped(idx),
        "offs2": striped(idx2),
    }


def reference(xt_words, xt_scales, wa, wb_words, wb_scales, offs, offs2):
    idx = unstriped(offs)
    idx2 = unstriped(offs2)
    xtu = unpack_weight(xt_words, xt_scales, "e4m3")
    wbu = unpack_weight(wb_words, wb_scales, "e2m1")
    waq = mxq(f64(wa), 0, "e4m3")
    xtidxg = xtu[:, idx]
    p = waq.T @ xtidxg
    xtidx2g = xtu[:, idx2]
    q = wbu.T @ xtidx2g
    y = p * q / (1.0 + np.abs(q))
    return y

@@ -1,0 +1,156 @@
+from contextlib import ExitStack
+
+import concourse.mybir as mybir
+
+K, T, J, N = 1024, 2048, 512, 512
+FLOPS = 2 * 2 * K * N * J
+
+F32 = mybir.dt.float32
+BF16 = mybir.dt.bfloat16
+I32 = mybir.dt.int32
+U32 = mybir.dt.uint32
+U16 = mybir.dt.uint16
+U8 = mybir.dt.uint8
+FP8X4 = mybir.dt.float8_e4m3fn_x4
+FP4X4 = mybir.dt.float4_e2m1fn_x4
+ACT = mybir.ActivationFunctionType
+MULT = mybir.AluOpType.mult
+
+P = 128
+PACK = 4
+K_PASS = P * PACK
+PASSES = K // K_PASS
+QUADS = 4
+M_TILE = 128
+TILES = N // M_TILE
+HALF = 256
+
+
+def tile_list_product_of_two_picks_kernel(tc, xt_words, xt_scales, wa, wb_words, wb_scales, offs, offs2, out):
+    nc = tc.nc
+    with ExitStack() as ctx:
+        keep = ctx.enter_context(tc.tile_pool(name="keep", bufs=1))
+        psum = ctx.enter_context(tc.psum_pool(name="psum", bufs=1))
+
+        list_p = keep.tile([P, J // 16], U16, name="list_p")
+        list_q = keep.tile([P, J // 16], U16, name="list_q")
+        xt_planes = keep.tile([P, T], U8, name="xt_planes", align_bytes=64)
+        wb_planes = keep.tile([P, PASSES, N], U8, name="wb_planes", align_bytes=64)
+        q_plane_1 = keep.tile([P, J], U8, name="q_plane_1", align_bytes=64)
+        nc.vector.memset(xt_planes[:].bitcast(I32), 0)
+        nc.vector.memset(wb_planes[:].bitcast(I32), 0)
+        nc.vector.memset(q_plane_1[:].bitcast(I32), 0)
+
+        nc.sync.dma_start(list_q[:], offs2)
+        nc.sync.dma_start(list_p[:], offs)
+        wb = keep.tile([P, PASSES, 2 * N], U8, name="wb", align_bytes=64)
+        nc.sync.dma_start(wb[:].bitcast(I32), wb_words.rearrange("a p c -> p a c").bitcast(I32))
+        for quad in range(QUADS):
+            nc.sync.dma_start(
+                xt_planes[32 * quad : 32 * quad + 4 * PASSES, :].bitcast(I32),
+                xt_scales[:, 4 * quad : 4 * quad + 4, :].bitcast(I32),
+            )
+        xt = [keep.tile([P, T], I32, name="xt%d" % a, align_bytes=64) for a in range(PASSES)]
+
+        def load_xt(a):
+            nc.sync.dma_start(xt[a][:], xt_words[a].rearrange("p c r -> p (c r)").bitcast(I32))
+
+        load_xt(0)
+        for quad in range(QUADS):
+            nc.sync.dma_start(
+                wb_planes[32 * quad : 32 * quad + 4, :, :].bitcast(I32),
+                wb_scales[:, 4 * quad : 4 * quad + 4, :].rearrange("a r c -> r a c").bitcast(I32),
+            )
+        load_xt(1)
+        pieces = [(h, a) for h in range(N // HALF) for a in range(PASSES)]
+        wa_raw = {}
+        for h, a in pieces:
+            wa_raw[h, a] = keep.tile([P, PACK, HALF], F32, name="wa_raw%d%d" % (h, a), align_bytes=64)
+            rows = wa[K_PASS * a : K_PASS * (a + 1), HALF * h : HALF * (h + 1)]
+            nc.sync.dma_start(wa_raw[h, a][:], rows.rearrange("(p r) c -> p r c", r=PACK))
+
+        q_planes = keep.tile([P, J], U8, name="q_planes", align_bytes=64)
+        p_planes = keep.tile([P, J], U8, name="p_planes", align_bytes=64)
+        nc.vector.tensor_copy(q_planes[:], xt_planes[:].indirect(list_q[:]))
+        last = 32 * (QUADS - 1) + 4
+        nc.scalar.dma_start(q_plane_1[0:last, :].bitcast(I32), q_planes[4 : last + 4, :].bitcast(I32))
+        nc.vector.tensor_copy(p_planes[:], xt_planes[:].indirect(list_p[:]))
+        xq = [keep.tile([P, J], U32, name="xq%d" % a, align_bytes=64) for a in range(PASSES)]
+        xp = [keep.tile([P, J], U32, name="xp%d" % a, align_bytes=64) for a in range(PASSES)]
+        q_acc = [psum.tile([P, J], F32, name="q_acc%d" % m) for m in range(TILES)]
+        p_acc = [psum.tile([P, J], F32, name="p_acc%d" % m) for m in range(TILES)]
+        q_scale = [q_planes, q_plane_1]
+        for a in range(PASSES):
+            nc.vector.tensor_copy(xq[a][:], xt[a][:].bitcast(U32).indirect(list_q[:]))
+            for m in range(TILES):
+                nc.tensor.matmul_mx(
+                    out=q_acc[m][:],
+                    lhsT=wb[:, a, 2 * M_TILE * m : 2 * M_TILE * (m + 1)].bitcast(FP4X4),
+                    lhsT_scale=wb_planes[:, a, M_TILE * m : M_TILE * (m + 1)],
+                    rhs=xq[a][:].bitcast(FP8X4),
+                    rhs_scale=q_scale[a][:],
+                    start=(a == 0),
+                    stop=(a == PASSES - 1),
+                )
+            nc.vector.tensor_copy(xp[a][:], xt[a][:].bitcast(U32).indirect(list_p[:]))
+
+        wa_bf, wa_codes, wa_plane = {}, {}, {}
+
+        def round_wa(h, a, copy):
+            wa_bf[h, a] = keep.tile([P, HALF, PACK], BF16, name="wa_bf%d%d" % (h, a), align_bytes=64)
+            copy(
+                wa_bf[h, a][:].rearrange("p (c i) r -> p c r i", i=4),
+                wa_raw[h, a][:].rearrange("p r (c i) -> p c r i", i=4),
+            )
+
+        def quantise_wa(h, a):
+            wa_codes[h, a] = keep.tile([P, HALF], U32, name="wa_codes%d%d" % (h, a), align_bytes=64)
+            wa_plane[h, a] = keep.tile([P, HALF], U8, name="wa_plane%d%d" % (h, a), align_bytes=64)
+            nc.vector.quantize_mx(
+                out=wa_codes[h, a][:].bitcast(FP8X4),
+                scales=wa_plane[h, a][:],
+                in_=wa_bf[h, a][:].rearrange("p c r -> p (c r)"),
+            )
+            for m in range(2 * h, 2 * h + 2):
+                cols = slice(M_TILE * (m % 2), M_TILE * (m % 2 + 1))
+                nc.tensor.matmul_mx(
+                    out=p_acc[m][:],
+                    lhsT=wa_codes[h, a][:, cols].bitcast(FP8X4),
+                    lhsT_scale=wa_plane[h, a][:, cols],
+                    rhs=xp[a][:].bitcast(FP8X4),
+                    rhs_scale=p_planes[4 * a : P, :],
+                    start=(a == 0),
+                    stop=(a == PASSES - 1),
+                )
+
+        mag = [keep.tile([P, J], F32, name="mag%d" % m) for m in range(TILES)]
+        root = [keep.tile([P, J], F32, name="root%d" % m) for m in range(TILES)]
+        inv = [keep.tile([P, J], F32, name="inv%d" % m) for m in range(TILES)]
+        gate = [keep.tile([P, J], F32, name="gate%d" % m) for m in range(TILES)]
+        res = [keep.tile([P, J], F32, name="res%d" % m) for m in range(TILES)]
+
+        round_wa(0, 0, nc.scalar.copy)
+        for step in range(TILES + 2):
+            if step < TILES:
+                nc.scalar.activation(mag[step][:], q_acc[step][:], ACT.Abs)
+            if 0 <= step - 1 < TILES:
+                nc.scalar.activation(root[step - 1][:], mag[step - 1][:], ACT.Abs_reciprocal_sqrt, bias=1.0)
+            if 0 <= step - 2 < TILES:
+                nc.scalar.activation(inv[step - 2][:], root[step - 2][:], ACT.Square)
+
+        def finish(m):
+            nc.vector.tensor_tensor(gate[m][:], q_acc[m][:], inv[m][:], MULT)
+            nc.vector.tensor_tensor(res[m][:], p_acc[m][:], gate[m][:], MULT)
+            nc.sync.dma_start(out[M_TILE * m : M_TILE * (m + 1), :], res[m][:])
+
+        round_wa(0, 1, nc.vector.tensor_copy)
+        quantise_wa(0, 0)
+        quantise_wa(0, 1)
+        round_wa(1, 0, nc.vector.tensor_copy)
+        finish(0)
+        quantise_wa(1, 0)
+        round_wa(1, 1, nc.vector.tensor_copy)
+        finish(1)
+        quantise_wa(1, 1)
+        finish(2)
+        finish(3)

@@ -42,20 +42,23 @@ def tile_list_product_of_two_picks_kernel(tc, xt_words, xt_scales, wa, wb_words,
         nc.vector.memset(q_plane_1[:].bitcast(I32), 0)
 
         nc.sync.dma_start(list_q[:], offs2)
-        nc.sync.dma_start(list_p[:], offs)
         wb = keep.tile([P, PASSES, 2 * N], U8, name="wb", align_bytes=64)
-        nc.sync.dma_start(wb[:].bitcast(I32), wb_words.rearrange("a p c -> p a c").bitcast(I32))
+        warm = keep.tile([P, 2], F32, name="warm")
+        nc.vector.memset(warm[:, 0:1], 1.0)
+        nc.scalar.activation(warm[:, 1:2], warm[:, 0:1], ACT.Abs_reciprocal_sqrt)
         for quad in range(QUADS):
             nc.sync.dma_start(
                 xt_planes[32 * quad : 32 * quad + 4 * PASSES, :].bitcast(I32),
                 xt_scales[:, 4 * quad : 4 * quad + 4, :].bitcast(I32),
             )
+        nc.sync.dma_start(list_p[:], offs)
         xt = [keep.tile([P, T], I32, name="xt%d" % a, align_bytes=64) for a in range(PASSES)]
 
         def load_xt(a):
             nc.sync.dma_start(xt[a][:], xt_words[a].rearrange("p c r -> p (c r)").bitcast(I32))
 
         load_xt(0)
+        nc.sync.dma_start(wb[:].bitcast(I32), wb_words.rearrange("a p c -> p a c").bitcast(I32))
         for quad in range(QUADS):
             nc.sync.dma_start(
                 wb_planes[32 * quad : 32 * quad + 4, :, :].bitcast(I32),
@@ -65,7 +68,7 @@ def tile_list_product_of_two_picks_kernel(tc, xt_words, xt_scales, wa, wb_words,
         pieces = [(h, a) for h in range(N // HALF) for a in range(PASSES)]
         wa_raw = {}
         for h, a in pieces:
-            wa_raw[h, a] = keep.tile([P, PACK, HALF], F32, name="wa_raw%d%d" % (h, a), align_bytes=64)
+            wa_raw[h, a] = keep.tile([P, PACK, HALF], F32, name="wa_raw%d%d" % (h, a), tag="wa_raw%d%d" % (h, a), align_bytes=64)
             rows = wa[K_PASS * a : K_PASS * (a + 1), HALF * h : HALF * (h + 1)]
             nc.sync.dma_start(wa_raw[h, a][:], rows.rearrange("(p r) c -> p r c", r=PACK))
 
@@ -96,11 +99,13 @@ def tile_list_product_of_two_picks_kernel(tc, xt_words, xt_scales, wa, wb_words,
 
         wa_bf, wa_codes, wa_plane = {}, {}, {}
 
-        def round_wa(h, a, copy):
+        for h, a in pieces:
             wa_bf[h, a] = keep.tile([P, HALF, PACK], BF16, name="wa_bf%d%d" % (h, a), align_bytes=64)
+
+        def round_wa(h, a, copy, cols=slice(0, HALF)):
             copy(
-                wa_bf[h, a][:].rearrange("p (c i) r -> p c r i", i=4),
-                wa_raw[h, a][:].rearrange("p r (c i) -> p c r i", i=4),
+                wa_bf[h, a][:, cols, :].rearrange("p (c i) r -> p c r i", i=4),
+                wa_raw[h, a][:, :, cols].rearrange("p r (c i) -> p c r i", i=4),
             )
 
         def quantise_wa(h, a):
@@ -123,34 +128,63 @@ def tile_list_product_of_two_picks_kernel(tc, xt_words, xt_scales, wa, wb_words,
                     stop=(a == PASSES - 1),
                 )
 
-        mag = [keep.tile([P, J], F32, name="mag%d" % m) for m in range(TILES)]
+        round_wa(0, 0, nc.scalar.copy)
+        mag = keep.tile([P, TILES, J], F32, name="mag", tag="wa_raw00", align_bytes=64)
         root = [keep.tile([P, J], F32, name="root%d" % m) for m in range(TILES)]
         inv = [keep.tile([P, J], F32, name="inv%d" % m) for m in range(TILES)]
         gate = [keep.tile([P, J], F32, name="gate%d" % m) for m in range(TILES)]
         res = [keep.tile([P, J], F32, name="res%d" % m) for m in range(TILES)]
+        whole = slice(0, J)
+        halves = [slice(0, J // 2), slice(J // 2, J)]
 
-        round_wa(0, 0, nc.scalar.copy)
-        for step in range(TILES + 2):
-            if step < TILES:
-                nc.scalar.activation(mag[step][:], q_acc[step][:], ACT.Abs)
-            if 0 <= step - 1 < TILES:
-                nc.scalar.activation(root[step - 1][:], mag[step - 1][:], ACT.Abs_reciprocal_sqrt, bias=1.0)
-            if 0 <= step - 2 < TILES:
-                nc.scalar.activation(inv[step - 2][:], root[step - 2][:], ACT.Square)
+        def magnitude(m):
+            nc.scalar.activation(mag[:, m, :], q_acc[m][:], ACT.Abs)
 
-        def finish(m):
-            nc.vector.tensor_tensor(gate[m][:], q_acc[m][:], inv[m][:], MULT)
-            nc.vector.tensor_tensor(res[m][:], p_acc[m][:], gate[m][:], MULT)
-            nc.sync.dma_start(out[M_TILE * m : M_TILE * (m + 1), :], res[m][:])
+        def inverse_root(m, cols=whole):
+            nc.scalar.activation(root[m][:, cols], mag[:, m, cols], ACT.Abs_reciprocal_sqrt, bias=1.0)
+
+        def square(m, cols=whole):
+            nc.scalar.activation(inv[m][:, cols], root[m][:, cols], ACT.Square)
+
+        magnitude(0)
+        magnitude(1)
+        inverse_root(0)
+        inverse_root(1)
+        square(0)
+        magnitude(2)
+        square(1)
+        round_wa(1, 1, nc.scalar.copy, slice(M_TILE, HALF))
+        inverse_root(2)
+        magnitude(3)
+        square(2)
+        for cols in halves:
+            inverse_root(3, cols)
+        for cols in halves:
+            square(3, cols)
+
+        def make_gate(m, cols):
+            nc.vector.tensor_tensor(gate[m][:, cols], q_acc[m][:, cols], inv[m][:, cols], MULT)
+
+        def make_result(m, cols):
+            nc.vector.tensor_tensor(res[m][:, cols], p_acc[m][:, cols], gate[m][:, cols], MULT)
+
+        def store(m, cols):
+            nc.sync.dma_start(out[M_TILE * m : M_TILE * (m + 1), cols], res[m][:, cols])
 
         round_wa(0, 1, nc.vector.tensor_copy)
         quantise_wa(0, 0)
-        quantise_wa(0, 1)
         round_wa(1, 0, nc.vector.tensor_copy)
-        finish(0)
+        quantise_wa(0, 1)
+        round_wa(1, 1, nc.vector.tensor_copy, slice(0, M_TILE))
         quantise_wa(1, 0)
-        round_wa(1, 1, nc.vector.tensor_copy)
-        finish(1)
-        quantise_wa(1, 1)
-        finish(2)
-        finish(3)
+        for m in range(TILES):
+            for cols in halves:
+                make_gate(m, cols)
+            if m == 1:
+                quantise_wa(1, 1)
+            for cols in halves:
+                make_result(m, cols)
+                if m == TILES - 1:
+                    store(m, cols)
+            if m < TILES - 1:
+                store(m, whole)

from contextlib import ExitStack

import concourse.mybir as mybir

K, T, J, N = 1024, 2048, 512, 512
FLOPS = 2 * 2 * K * N * J

F32 = mybir.dt.float32
BF16 = mybir.dt.bfloat16
I32 = mybir.dt.int32
U32 = mybir.dt.uint32
U16 = mybir.dt.uint16
U8 = mybir.dt.uint8
FP8X4 = mybir.dt.float8_e4m3fn_x4
FP4X4 = mybir.dt.float4_e2m1fn_x4
ACT = mybir.ActivationFunctionType
MULT = mybir.AluOpType.mult

P = 128
PACK = 4
K_PASS = P * PACK
PASSES = K // K_PASS
QUADS = 4
M_TILE = 128
TILES = N // M_TILE
HALF = 256


def tile_list_product_of_two_picks_kernel(tc, xt_words, xt_scales, wa, wb_words, wb_scales, offs, offs2, out):
    nc = tc.nc
    with ExitStack() as ctx:
        keep = ctx.enter_context(tc.tile_pool(name="keep", bufs=1))
        psum = ctx.enter_context(tc.psum_pool(name="psum", bufs=1))

        list_p = keep.tile([P, J // 16], U16, name="list_p")
        list_q = keep.tile([P, J // 16], U16, name="list_q")
        xt_planes = keep.tile([P, T], U8, name="xt_planes", align_bytes=64)
        wb_planes = keep.tile([P, PASSES, N], U8, name="wb_planes", align_bytes=64)
        q_plane_1 = keep.tile([P, J], U8, name="q_plane_1", align_bytes=64)
        nc.vector.memset(xt_planes[:].bitcast(I32), 0)
        nc.vector.memset(wb_planes[:].bitcast(I32), 0)
        nc.vector.memset(q_plane_1[:].bitcast(I32), 0)

        nc.sync.dma_start(list_q[:], offs2)
        wb = keep.tile([P, PASSES, 2 * N], U8, name="wb", align_bytes=64)
        warm = keep.tile([P, 2], F32, name="warm")
        nc.vector.memset(warm[:, 0:1], 1.0)
        nc.scalar.activation(warm[:, 1:2], warm[:, 0:1], ACT.Abs_reciprocal_sqrt)
        for quad in range(QUADS):
            nc.sync.dma_start(
                xt_planes[32 * quad : 32 * quad + 4 * PASSES, :].bitcast(I32),
                xt_scales[:, 4 * quad : 4 * quad + 4, :].bitcast(I32),
            )
        nc.sync.dma_start(list_p[:], offs)
        xt = [keep.tile([P, T], I32, name="xt%d" % a, align_bytes=64) for a in range(PASSES)]

        def load_xt(a):
            nc.sync.dma_start(xt[a][:], xt_words[a].rearrange("p c r -> p (c r)").bitcast(I32))

        load_xt(0)
        nc.sync.dma_start(wb[:].bitcast(I32), wb_words.rearrange("a p c -> p a c").bitcast(I32))
        for quad in range(QUADS):
            nc.sync.dma_start(
                wb_planes[32 * quad : 32 * quad + 4, :, :].bitcast(I32),
                wb_scales[:, 4 * quad : 4 * quad + 4, :].rearrange("a r c -> r a c").bitcast(I32),
            )
        load_xt(1)
        pieces = [(h, a) for h in range(N // HALF) for a in range(PASSES)]
        wa_raw = {}
        for h, a in pieces:
            wa_raw[h, a] = keep.tile([P, PACK, HALF], F32, name="wa_raw%d%d" % (h, a), tag="wa_raw%d%d" % (h, a), align_bytes=64)
            rows = wa[K_PASS * a : K_PASS * (a + 1), HALF * h : HALF * (h + 1)]
            nc.sync.dma_start(wa_raw[h, a][:], rows.rearrange("(p r) c -> p r c", r=PACK))

        q_planes = keep.tile([P, J], U8, name="q_planes", align_bytes=64)
        p_planes = keep.tile([P, J], U8, name="p_planes", align_bytes=64)
        nc.vector.tensor_copy(q_planes[:], xt_planes[:].indirect(list_q[:]))
        last = 32 * (QUADS - 1) + 4
        nc.scalar.dma_start(q_plane_1[0:last, :].bitcast(I32), q_planes[4 : last + 4, :].bitcast(I32))
        nc.vector.tensor_copy(p_planes[:], xt_planes[:].indirect(list_p[:]))
        xq = [keep.tile([P, J], U32, name="xq%d" % a, align_bytes=64) for a in range(PASSES)]
        xp = [keep.tile([P, J], U32, name="xp%d" % a, align_bytes=64) for a in range(PASSES)]
        q_acc = [psum.tile([P, J], F32, name="q_acc%d" % m) for m in range(TILES)]
        p_acc = [psum.tile([P, J], F32, name="p_acc%d" % m) for m in range(TILES)]
        q_scale = [q_planes, q_plane_1]
        for a in range(PASSES):
            nc.vector.tensor_copy(xq[a][:], xt[a][:].bitcast(U32).indirect(list_q[:]))
            for m in range(TILES):
                nc.tensor.matmul_mx(
                    out=q_acc[m][:],
                    lhsT=wb[:, a, 2 * M_TILE * m : 2 * M_TILE * (m + 1)].bitcast(FP4X4),
                    lhsT_scale=wb_planes[:, a, M_TILE * m : M_TILE * (m + 1)],
                    rhs=xq[a][:].bitcast(FP8X4),
                    rhs_scale=q_scale[a][:],
                    start=(a == 0),
                    stop=(a == PASSES - 1),
                )
            nc.vector.tensor_copy(xp[a][:], xt[a][:].bitcast(U32).indirect(list_p[:]))

        wa_bf, wa_codes, wa_plane = {}, {}, {}

        for h, a in pieces:
            wa_bf[h, a] = keep.tile([P, HALF, PACK], BF16, name="wa_bf%d%d" % (h, a), align_bytes=64)

        def round_wa(h, a, copy, cols=slice(0, HALF)):
            copy(
                wa_bf[h, a][:, cols, :].rearrange("p (c i) r -> p c r i", i=4),
                wa_raw[h, a][:, :, cols].rearrange("p r (c i) -> p c r i", i=4),
            )

        def quantise_wa(h, a):
            wa_codes[h, a] = keep.tile([P, HALF], U32, name="wa_codes%d%d" % (h, a), align_bytes=64)
            wa_plane[h, a] = keep.tile([P, HALF], U8, name="wa_plane%d%d" % (h, a), align_bytes=64)
            nc.vector.quantize_mx(
                out=wa_codes[h, a][:].bitcast(FP8X4),
                scales=wa_plane[h, a][:],
                in_=wa_bf[h, a][:].rearrange("p c r -> p (c r)"),
            )
            for m in range(2 * h, 2 * h + 2):
                cols = slice(M_TILE * (m % 2), M_TILE * (m % 2 + 1))
                nc.tensor.matmul_mx(
                    out=p_acc[m][:],
                    lhsT=wa_codes[h, a][:, cols].bitcast(FP8X4),
                    lhsT_scale=wa_plane[h, a][:, cols],
                    rhs=xp[a][:].bitcast(FP8X4),
                    rhs_scale=p_planes[4 * a : P, :],
                    start=(a == 0),
                    stop=(a == PASSES - 1),
                )

        round_wa(0, 0, nc.scalar.copy)
        mag = keep.tile([P, TILES, J], F32, name="mag", tag="wa_raw00", align_bytes=64)
        root = [keep.tile([P, J], F32, name="root%d" % m) for m in range(TILES)]
        inv = [keep.tile([P, J], F32, name="inv%d" % m) for m in range(TILES)]
        gate = [keep.tile([P, J], F32, name="gate%d" % m) for m in range(TILES)]
        res = [keep.tile([P, J], F32, name="res%d" % m) for m in range(TILES)]
        whole = slice(0, J)
        halves = [slice(0, J // 2), slice(J // 2, J)]

        def magnitude(m):
            nc.scalar.activation(mag[:, m, :], q_acc[m][:], ACT.Abs)

        def inverse_root(m, cols=whole):
            nc.scalar.activation(root[m][:, cols], mag[:, m, cols], ACT.Abs_reciprocal_sqrt, bias=1.0)

        def square(m, cols=whole):
            nc.scalar.activation(inv[m][:, cols], root[m][:, cols], ACT.Square)

        magnitude(0)
        magnitude(1)
        inverse_root(0)
        inverse_root(1)
        square(0)
        magnitude(2)
        square(1)
        round_wa(1, 1, nc.scalar.copy, slice(M_TILE, HALF))
        inverse_root(2)
        magnitude(3)
        square(2)
        for cols in halves:
            inverse_root(3, cols)
        for cols in halves:
            square(3, cols)

        def make_gate(m, cols):
            nc.vector.tensor_tensor(gate[m][:, cols], q_acc[m][:, cols], inv[m][:, cols], MULT)

        def make_result(m, cols):
            nc.vector.tensor_tensor(res[m][:, cols], p_acc[m][:, cols], gate[m][:, cols], MULT)

        def store(m, cols):
            nc.sync.dma_start(out[M_TILE * m : M_TILE * (m + 1), cols], res[m][:, cols])

        round_wa(0, 1, nc.vector.tensor_copy)
        quantise_wa(0, 0)
        round_wa(1, 0, nc.vector.tensor_copy)
        quantise_wa(0, 1)
        round_wa(1, 1, nc.vector.tensor_copy, slice(0, M_TILE))
        quantise_wa(1, 0)
        for m in range(TILES):
            for cols in halves:
                make_gate(m, cols)
            if m == 1:
                quantise_wa(1, 1)
            for cols in halves:
                make_result(m, cols)
                if m == TILES - 1:
                    store(m, cols)
            if m < TILES - 1:
                store(m, whole)
